import numpy as np
import ml_dtypes


def mxq(x, axis, fmt="e4m3"):
    dtype, down = {"e4m3": (ml_dtypes.float8_e4m3fn, 7), "e5m2": (ml_dtypes.float8_e5m2, 14)}[fmt]
    v = np.moveaxis(np.asarray(x, np.float32).astype(ml_dtypes.bfloat16).astype(np.float64), axis, -1)
    blocks = v.reshape(v.shape[:-1] + (-1, 32))
    amax = np.abs(blocks).max(-1, keepdims=True)
    byte = np.maximum(np.where(amax > 0, np.frexp(amax)[1] - 1 + 127, 0) - down, 1)
    scale = np.exp2(byte - 127.0)
    codes = (blocks / scale).astype(np.float32).astype(dtype).astype(np.float64)
    return np.moveaxis((codes * scale).reshape(v.shape), -1, axis)


WIDE = False


def mx_kscale(k):
    if not WIDE:
        return np.ones(k)
    levels = np.array([10, -10, 5, -5, 0])
    if k % 512:
        return np.exp2(np.random.permutation(np.resize(levels, k // 32))).repeat(32)
    a = np.empty((k // 512, 16))
    for p in range(k // 512):
        a[p, :8] = np.random.permutation(np.resize(levels, 8))
        for g in range(8):
            far = levels[np.abs(levels - a[p, g]) >= 10]
            a[p, g + 8] = far[np.random.randint(len(far))]
    return np.exp2(a.ravel()).repeat(32)


def f64(x):
    return np.asarray(x).astype(np.float64)


def striped(idx):
    return np.tile(idx.reshape(-1, 16).T, (8, 1)).astype(np.uint16)


def unstriped(offs):
    return offs[:16].T.reshape(-1).astype(np.int64)


E2M1 = np.array([0.0, 0.5, 1.0, 1.5, 2.0, 3.0, 4.0, 6.0, -0.0, -0.5, -1.0, -1.5, -2.0, -3.0, -4.0, -6.0])


def pack_weight(w, fmt):
    k, n = w.shape
    w = f64(np.asarray(w, np.float32).astype(ml_dtypes.bfloat16)).reshape(k // 32, 32, n)
    amax = np.abs(w).max(1)
    if fmt == "e4m3":
        byte = np.frexp(amax)[1] - 1 + 127 - 7
    else:
        mant, ex = np.frexp(amax / 6.0)
        byte = np.where(mant > 0.5, ex, ex - 1) + 127
    byte = np.clip(np.where(amax > 0, byte, 1), 1, 254)
    scaled = (w * np.exp2(127.0 - byte)[:, None, :]).reshape(k, n).astype(np.float32)
    by_word = np.ascontiguousarray(scaled.reshape(k // 512, 128, 4, n).transpose(0, 1, 3, 2))
    if fmt == "e4m3":
        words = by_word.astype(ml_dtypes.float8_e4m3fn).view(np.uint8)
    else:
        c = by_word.astype(ml_dtypes.float4_e2m1fn).view(np.uint8) & 0xF
        words = (c[..., 0::2] | (c[..., 1::2] << 4)).reshape(k // 512, 128, 2 * n)
    return np.ascontiguousarray(words), np.ascontiguousarray(byte.astype(np.uint8).reshape(k // 512, 16, n))


def unpack_weight(words, scales, fmt):
    g, _, n = scales.shape
    words = np.ascontiguousarray(words).reshape(g, 128, n, -1)
    if fmt == "e4m3":
        vals = words.view(ml_dtypes.float8_e4m3fn).astype(np.float64)
    else:
        nib = np.empty((g, 128, n, 4), np.uint8)
        nib[..., 0::2] = words & 0xF
        nib[..., 1::2] = words >> 4
        vals = E2M1[nib]
    vals = vals * np.repeat(np.exp2(scales.astype(np.float64) - 127.0), 8, axis=1)[..., None]
    return vals.transpose(0, 1, 3, 2).reshape(g * 512, n)


def gelu(v):
    return 0.5 * v * (1.0 + np.tanh(np.sqrt(2.0 / np.pi) * (v + 0.044715 * v**3)))


K, H, N, T, S, P, P2 = 1536, 1024, 768, 4096, 1024, 512, 256


def setup_inputs():
    n = np.random.standard_normal
    s = mx_kscale(K)[:, None]
    u = mx_kscale(H)[:, None]
    tab_words, tab_scales = pack_weight(n((K, T)) * s, "e4m3")
    w4_words, w4_scales = pack_weight(1.3 * n((K, H)) / np.sqrt(K) / s, "e2m1")
    gauges = np.random.permutation(S)
    return {
        "tab_words": tab_words,
        "tab_scales": tab_scales,
        "offs": striped(np.random.permutation(T)[:S]),
        "w4_words": w4_words,
        "w4_scales": w4_scales,
        "gain": (np.exp(0.3 * n(H)) * u[:, 0]).astype(np.float32),
        "pos1": striped(gauges[:P]),
        "pos2": striped(gauges[S - P:]),
        "w2": (1.4 * n((H, N)) / np.sqrt(H) / u).astype(np.float32),
        "pos3": striped(np.random.permutation(P)[:P2]),
        "pos4": striped(np.random.permutation(P)[:P2]),
        "town": (0.7 * n((N, P2))).astype(np.float32),
    }


def reference(tab_words, tab_scales, offs, w4_words, w4_scales, gain, pos1, pos2, w2, pos3, pos4, town):
    v = unpack_weight(tab_words, tab_scales, "e4m3")[:, unstriped(offs)]
    w4 = unpack_weight(w4_words, w4_scales, "e2m1")
    h = np.tanh(w4.T @ v) * f64(gain)[:, None]
    d = np.abs(h[:, unstriped(pos1)] - h[:, unstriped(pos2)])
    y = mxq(f64(w2), 0, "e4m3").T @ mxq(d, 0, "e4m3")
    return np.tanh(y[:, unstriped(pos3)]) * y[:, unstriped(pos4)] + f64(town)

from contextlib import ExitStack

import concourse.mybir as mybir
from concourse.masks import make_identity

K, H, N, T, S, PAIRS, TOWNS = 1536, 1024, 768, 4096, 1024, 512, 256
FLOPS = 2 * K * H * S + 2 * H * N * PAIRS

F32 = mybir.dt.float32
BF16 = mybir.dt.bfloat16
I32 = mybir.dt.int32
U32 = mybir.dt.uint32
U16 = mybir.dt.uint16
U8 = mybir.dt.uint8
FP8X4 = mybir.dt.float8_e4m3fn_x4
FP4X4 = mybir.dt.float4_e2m1fn_x4
ACT = mybir.ActivationFunctionType
ALU = mybir.AluOpType

P = 128
PASSES1 = K // 512
PASSES2 = H // 512
BANK = 512
NSLICES = N // P
ROOM = 4 * T
SROWS = 16 * PASSES1


def tile_list_river_crest_pairs_kernel(
    tc, tab_words, tab_scales, offs, w4_words, w4_scales, gain, pos1, pos2, w2, pos3, pos4, town, out
):
    nc = tc.nc
    with ExitStack() as ctx:
        keep = ctx.enter_context(tc.tile_pool(name="keep", bufs=1))
        ring = ctx.enter_context(tc.tile_pool(name="ring", bufs=3))
        big = ctx.enter_context(tc.tile_pool(name="big", bufs=1))
        psum = ctx.enter_context(tc.psum_pool(name="psum", bufs=8))

        def list_tile(src, name):
            t = keep.tile([P, src.shape[1]], U16, name=name)
            nc.sync.dma_start(t[:], src)
            return t

        def load_table(a):
            t = big.tile([P, T], U32, name="tab%d" % a, align_bytes=64, offset=ROOM * a)
            nc.sync.dma_start(t[:].bitcast(I32), tab_words[a].rearrange("p t i -> p (t i)").bitcast(I32))
            return t

        def load_w4(b, t):
            nc.sync.dma_start(
                t[:].bitcast(I32),
                w4_words[:, :, 1024 * b : 1024 * (b + 1)].rearrange("a p c -> p a c").bitcast(I32),
            )
            return t

        offs_t = list_tile(offs, "offs_t")
        w4raw = [load_w4(0, keep.tile([P, PASSES1, 1024], U8, name="w4raw0", align_bytes=64))]
        w4sraw = big.tile([P, H], U8, name="w4sraw", align_bytes=64, offset=ROOM)
        nc.sync.dma_start(w4sraw[0:SROWS, :].bitcast(I32), w4_scales.rearrange("a q c -> q a c").bitcast(I32))
        tab = [load_table(0)]
        pos1_t = list_tile(pos1, "pos1_t")
        pos2_t = list_tile(pos2, "pos2_t")
        pos3_t = list_tile(pos3, "pos3_t")
        pos4_t = list_tile(pos4, "pos4_t")

        swin = keep.tile([P, T], U8, name="swin", tag="wide0", align_bytes=64)
        nc.vector.memset(swin[:].bitcast(I32), 0)
        nc.scalar.dma_start(swin[0:SROWS, :].bitcast(I32), tab_scales.rearrange("a q t -> q a t").bitcast(I32))
        planes = keep.tile([P, PASSES1, 2, S], U8, name="planes", align_bytes=64)
        nc.vector.memset(planes[:].bitcast(I32), 0)
        stage = keep.tile([P, 2, S], U8, name="stage", align_bytes=64)
        nc.vector.tensor_copy(
            stage[0:SROWS, 1, :].bitcast(I32).rearrange("p (b t q w) -> p b t q w", b=2, t=4, w=2),
            w4sraw[0:SROWS, :].bitcast(I32).rearrange("p (b q t w) -> p b t q w", b=2, t=4, w=2),
        )
        tab.append(load_table(1))
        sgath = big.tile([P, S], U8, name="sgath", align_bytes=64, offset=2 * ROOM)
        nc.vector.tensor_copy(sgath[:], swin[:].indirect(offs_t[:]))
        nc.vector.tensor_copy(stage[0:SROWS, 0, :].bitcast(I32), sgath[0:SROWS, :].bitcast(I32))
        for q in range(4):
            nc.sync.dma_start(
                planes[32 * q : 32 * q + 4].bitcast(I32), stage[12 * q : 12 * (q + 1)].bitcast(I32)
            )
        tab.append(load_table(2))

        gstage = keep.tile([P, P], F32, name="gstage")
        nc.vector.memset(gstage[:], 0.0)
        for b in range(PASSES2):
            nc.gpsimd.dma_start(
                gstage[4 * b : 4 * b + 4, :],
                gain[512 * b : 512 * (b + 1)].rearrange("(q t i) -> t q i", t=4, i=8),
            )
        ident = keep.tile([P, P], F32, name="ident")
        make_identity(nc, ident[:])
        gps = psum.tile([P, P], F32, name="gps", tag="bank")
        nc.tensor.transpose(gps[:], gstage[:], ident[:])
        gcol = keep.tile([P, 8], F32, name="gcol")
        nc.scalar.copy(gcol[:], gps[:, 0:8])

        def deal_w4(b):
            t = keep.tile([P, PASSES1, 1024], U8, name="w4w%d" % b, align_bytes=64)
            nc.vector.tensor_copy(
                t[:].bitcast(I32).rearrange("p a (t q w) -> p a t q w", t=4, w=4),
                w4raw[b][:].bitcast(I32).rearrange("p a (q t w) -> p a t q w", t=4, w=4),
            )
            return t

        def load_w2(b):
            t = big.tile([P, 4, N], F32, name="w2raw%d" % b, align_bytes=64, offset=ROOM * b)
            rows = w2[512 * b : 512 * (b + 1), :].rearrange("(q t i) n -> t q i n", t=4, i=8)
            for s in range(4):
                nc.sync.dma_start(t[:, s, :], rows[s])
            return t

        w4w = [deal_w4(0)]
        vw = []
        for a in range(PASSES1):
            vw.append(keep.tile([P, S], U32, name="vw%d" % a, tag="wide%d" % a, align_bytes=64))
        nc.vector.tensor_copy(vw[0][:], tab[0][:].indirect(offs_t[:]))
        w4raw.append(load_w4(1, big.tile([P, PASSES1, 1024], U8, name="w4raw1", align_bytes=64, offset=16 * N)))
        w2raw = [load_w2(0)]
        nc.vector.tensor_copy(vw[1][:], tab[1][:].indirect(offs_t[:]))
        w2raw.append(load_w2(1))
        for hf in range(2):
            nc.vector.tensor_copy(
                vw[2][:, BANK * hf : BANK * (hf + 1)], tab[2][:].indirect(offs_t[:, 32 * hf : 32 * (hf + 1)])
            )
        town_t = big.tile([P, NSLICES, TOWNS], F32, name="town_t", align_bytes=64, offset=2 * ROOM)
        nc.sync.dma_start(town_t[:], town.rearrange("(s p) j -> p s j", p=P))
        w4w.append(deal_w4(1))

        th = []
        for s in range(8):
            b, t = divmod(s, 4)
            tile_h = keep.tile([P, S], F32, name="th%d" % s, align_bytes=64)
            for hf in range(2):
                cols = slice(BANK * hf, BANK * (hf + 1))
                acc = psum.tile([P, BANK], F32, name="acc", tag="bank")
                for a in range(PASSES1):
                    nc.tensor.matmul_mx(
                        out=acc[:],
                        lhsT=w4w[b][:, a, 256 * t : 256 * (t + 1)].bitcast(FP4X4),
                        lhsT_scale=planes[:, a, 1, P * s : P * (s + 1)],
                        rhs=vw[a][:, cols].bitcast(FP8X4),
                        rhs_scale=planes[:, a, 0, cols],
                        start=(a == 0),
                        stop=(a == PASSES1 - 1),
                    )
                nc.scalar.activation(tile_h[:, cols], acc[:], ACT.Tanh)
            th.append(tile_h)

        w2q = {}

        def quantise_w2(b, n0, width):
            name = "w2_%d_%d" % (b, n0)
            woven = keep.tile([P, width * 4], BF16, name=name + "b", align_bytes=64)
            nc.scalar.copy(
                woven[:].rearrange("p (c i t) -> p c t i", i=4, t=4),
                w2raw[b][:, :, n0 : n0 + width].rearrange("p t (c i) -> p c t i", i=4),
            )
            codes = keep.tile([P, width], U32, name=name + "c", align_bytes=64)
            scales = keep.tile([P, width], U8, name=name + "s", align_bytes=64)
            nc.vector.quantize_mx(out=codes[:].bitcast(FP8X4), scales=scales[:], in_=woven[:])
            for j in range(width // P):
                w2q[(b, n0 // P + j)] = (codes[:, P * j : P * (j + 1)], scales[:, P * j : P * (j + 1)])

        for n0 in (0, 256):
            for b in range(PASSES2):
                quantise_w2(b, n0, 256)

        HALF = PAIRS // 2
        dq = []
        ybank = {}

        def second_pass(b, n):
            if b == 0:
                ybank[n] = psum.tile([P, PAIRS], F32, name="yacc%d" % n, tag="bank")
            nc.tensor.matmul_mx(
                out=ybank[n][:],
                lhsT=w2q[(b, n)][0].bitcast(FP8X4),
                lhsT_scale=w2q[(b, n)][1],
                rhs=dq[b][0][:].bitcast(FP8X4),
                rhs_scale=dq[b][1][:],
                start=(b == 0),
                stop=(b == PASSES2 - 1),
            )

        for b in range(PASSES2):
            dabs = keep.tile([P, 2, 4, HALF], BF16, name="dabs%d" % b, align_bytes=64)
            for t in range(4):
                s = 4 * b + t
                first = []
                for hf in range(2):
                    g = ring.tile([P, HALF], F32, name="g1", tag="g1", bufs=4, align_bytes=64)
                    nc.vector.tensor_copy(g[:], th[s][:].indirect(pos1_t[:, 16 * hf : 16 * (hf + 1)]))
                    first.append(g)
                for hf in range(2):
                    diff = keep.tile([P, HALF], F32, name="diff%d_%d" % (s, hf), align_bytes=64)
                    nc.vector.tensor_tensor(
                        diff[:], th[s][:].indirect(pos2_t[:, 16 * hf : 16 * (hf + 1)]), first[hf][:], ALU.subtract
                    )
                    nc.scalar.activation(dabs[:, hf, t, :], diff[:], ACT.Abs, scale=gcol[:, s : s + 1])
            woven = keep.tile([P, 2, HALF * 4], BF16, name="dwoven%d" % b, align_bytes=64)
            codes = keep.tile([P, PAIRS], U32, name="dcodes%d" % b, align_bytes=64)
            scales = keep.tile([P, PAIRS], U8, name="dscales%d" % b, align_bytes=64)
            for hf in range(2):
                dst = woven[:, hf, :].rearrange("p (c i t) -> p c t i", i=4, t=4)
                src = dabs[:, hf].rearrange("p t (c i) -> p c t i", i=4)
                if b == 0:
                    nc.scalar.copy(dst, src)
                else:
                    nc.vector.tensor_copy(dst, src)
            for hf in range(2):
                cols = slice(HALF * hf, HALF * (hf + 1))
                nc.vector.quantize_mx(out=codes[:, cols].bitcast(FP8X4), scales=scales[:, cols], in_=woven[:, hf, :])
            dq.append((codes, scales))
            if b == 0:
                for n in range(4):
                    second_pass(0, n)

        ys = {}
        QUARTER = TOWNS // 2

        def bring_y(n):
            if n >= 4:
                for b in range(PASSES2):
                    quantise_w2(b, P * n, P)
                second_pass(0, n)
            second_pass(1, n)
            y = keep.tile([P, PAIRS], F32, name="y", tag="wide%d" % (n % 3), align_bytes=64)
            nc.scalar.copy(y[:], ybank[n][:])
            g3 = ring.tile([P, TOWNS], F32, name="g3", tag="g3", align_bytes=64)
            nc.vector.tensor_copy(g3[:], y[:].indirect(pos3_t[:]))
            ys[n] = (y, g3)

        def finish(n):
            y, g3 = ys[n]
            t3 = ring.tile([P, TOWNS], F32, name="t3", tag="t3", align_bytes=64)
            nc.scalar.activation(t3[:], g3[:], ACT.Tanh)
            prod = ring.tile([P, TOWNS], F32, name="prod", tag="prod", align_bytes=64)
            res = keep.tile([P, TOWNS], F32, name="res%d" % n, align_bytes=64)
            for hf in range(2):
                cols = slice(QUARTER * hf, QUARTER * (hf + 1))
                nc.vector.tensor_tensor(
                    prod[:, cols], y[:].indirect(pos4_t[:, 8 * hf : 8 * (hf + 1)]), t3[:, cols], ALU.mult
                )
            for hf in range(2):
                cols = slice(QUARTER * hf, QUARTER * (hf + 1))
                nc.vector.tensor_tensor(res[:, cols], prod[:, cols], town_t[:, n, cols], ALU.add)
            nc.sync.dma_start(out[P * n : P * (n + 1), :], res[:])

        bring_y(0)
        for n in range(NSLICES):
            if n + 1 < NSLICES:
                bring_y(n + 1)
            finish(n)
